import numpy as np
import ml_dtypes

BF16 = ml_dtypes.bfloat16


def bf(x):
    return np.asarray(x, np.float32).astype(BF16)


def f32(x):
    return np.asarray(x, np.float32)


def f64(x):
    return np.asarray(x).astype(np.float64)


def striped(idx):
    return np.tile(idx.reshape(-1, 16).T, (8, 1))


def rows(idx, k):
    return np.tile(idx, (k, 1))


def look(tab, idx):
    return np.take_along_axis(f64(tab), rows(idx, len(tab)), axis=1)


K, S, V, N = 256, 2048, 512, 512


def setup_inputs():
    return {"tab": f32(np.random.standard_normal((2, K, S))), "offs": striped(np.random.permutation(S)[:N])}


def reference(tab, offs):
    idx = offs[:16].T.reshape(-1)
    x = (look(tab[0], idx) >= 0.25) * 0.5 * np.tanh(look(tab[1], idx))
    return x

@@ -1,0 +1,51 @@
+import concourse.mybir as mybir
+
+F32, U16 = mybir.dt.float32, mybir.dt.uint16
+ALU = mybir.AluOpType
+TANH = mybir.ActivationFunctionType.Tanh
+
+P = 128
+THRESHOLD = 0.25
+GAIN = 0.5
+PIECES = 2
+
+
+def tile_lookup_steptanh_out_kernel(tc, tab, offs, out):
+    nc = tc.nc
+    places = tab.shape[2]
+    n = out.shape[1]
+    blocks = tab.shape[1] // P
+
+    with (
+        tc.tile_pool(name="list", bufs=1) as list_pool,
+        tc.tile_pool(name="tables", bufs=blocks) as tables,
+        tc.tile_pool(name="work", bufs=PIECES * blocks) as work,
+    ):
+        offsets = list_pool.tile([P, offs.shape[1]], U16, name="offsets")
+        nc.sync.dma_start(offsets[:], offs)
+
+        values, keys = [], []
+        for b in range(blocks):
+            rows = slice(b * P, (b + 1) * P)
+            key_tile = tables.tile([P, places], F32, name="key_tile")
+            nc.sync.dma_start(key_tile[:], tab[0, rows, :])
+            value_tile = tables.tile([P, places], F32, name="value_tile")
+            nc.sync.dma_start(value_tile[:], tab[1, rows, :])
+            values.append(value_tile)
+            keys.append(key_tile)
+
+        width = n // PIECES
+        for b in range(blocks):
+            rows = slice(b * P, (b + 1) * P)
+            for piece in range(PIECES):
+                columns = slice(piece * width, (piece + 1) * width)
+                entries = offsets[:, piece * width // 16 : (piece + 1) * width // 16]
+                squashed = work.tile([P, width], F32, name="squashed")
+                nc.scalar.activation(squashed[:], values[b][:].indirect(entries), TANH)
+                step = work.tile([P, width], F32, name="step")
+                nc.vector.tensor_scalar(
+                    step[:], keys[b][:].indirect(entries), THRESHOLD, GAIN, op0=ALU.is_ge, op1=ALU.mult
+                )
+                x = work.tile([P, width], F32, name="x")
+                nc.vector.tensor_tensor(x[:], step[:], squashed[:], op=ALU.mult)
+                nc.sync.dma_start(out[rows, columns], x[:])

@@ -5,9 +5,10 @@ ALU = mybir.AluOpType
 TANH = mybir.ActivationFunctionType.Tanh
 
 P = 128
+GROUP = 16
 THRESHOLD = 0.25
 GAIN = 0.5
-PIECES = 2
+LAST_PIECES = (256, 128, 128)
 
 
 def tile_lookup_steptanh_out_kernel(tc, tab, offs, out):
@@ -19,33 +20,35 @@ def tile_lookup_steptanh_out_kernel(tc, tab, offs, out):
     with (
         tc.tile_pool(name="list", bufs=1) as list_pool,
         tc.tile_pool(name="tables", bufs=blocks) as tables,
-        tc.tile_pool(name="work", bufs=PIECES * blocks) as work,
+        tc.tile_pool(name="work", bufs=blocks) as work,
     ):
         offsets = list_pool.tile([P, offs.shape[1]], U16, name="offsets")
-        nc.sync.dma_start(offsets[:], offs)
 
         values, keys = [], []
         for b in range(blocks):
             rows = slice(b * P, (b + 1) * P)
             key_tile = tables.tile([P, places], F32, name="key_tile")
             nc.sync.dma_start(key_tile[:], tab[0, rows, :])
+            if b == 0:
+                nc.sync.dma_start(offsets[:], offs)
             value_tile = tables.tile([P, places], F32, name="value_tile")
             nc.sync.dma_start(value_tile[:], tab[1, rows, :])
             values.append(value_tile)
             keys.append(key_tile)
 
-        width = n // PIECES
         for b in range(blocks):
             rows = slice(b * P, (b + 1) * P)
-            for piece in range(PIECES):
-                columns = slice(piece * width, (piece + 1) * width)
-                entries = offsets[:, piece * width // 16 : (piece + 1) * width // 16]
-                squashed = work.tile([P, width], F32, name="squashed")
-                nc.scalar.activation(squashed[:], values[b][:].indirect(entries), TANH)
-                step = work.tile([P, width], F32, name="step")
-                nc.vector.tensor_scalar(
-                    step[:], keys[b][:].indirect(entries), THRESHOLD, GAIN, op0=ALU.is_ge, op1=ALU.mult
-                )
-                x = work.tile([P, width], F32, name="x")
-                nc.vector.tensor_tensor(x[:], step[:], squashed[:], op=ALU.mult)
-                nc.sync.dma_start(out[rows, columns], x[:])
+            step = work.tile([P, n], F32, name="step")
+            nc.vector.tensor_scalar(
+                step[:], keys[b][:].indirect(offsets[:]), THRESHOLD, GAIN, op0=ALU.is_ge, op1=ALU.mult
+            )
+            squashed = work.tile([P, n], F32, name="squashed")
+            x = work.tile([P, n], F32, name="x")
+            start = 0
+            for width in LAST_PIECES if b == blocks - 1 else (n,):
+                columns = slice(start, start + width)
+                entries = offsets[:, start // GROUP : (start + width) // GROUP]
+                nc.scalar.activation(squashed[:, columns], values[b][:].indirect(entries), TANH)
+                nc.vector.tensor_tensor(x[:, columns], step[:, columns], squashed[:, columns], op=ALU.mult)
+                nc.sync.dma_start(out[rows, columns], x[:, columns])
+                start += width

@@ -50,5 +50,6 @@ def tile_lookup_steptanh_out_kernel(tc, tab, offs, out):
                 entries = offsets[:, start // GROUP : (start + width) // GROUP]
                 nc.scalar.activation(squashed[:, columns], values[b][:].indirect(entries), TANH)
                 nc.vector.tensor_tensor(x[:, columns], step[:, columns], squashed[:, columns], op=ALU.mult)
-                nc.sync.dma_start(out[rows, columns], x[:, columns])
                 start += width
+                queue = nc.scalar if b == blocks - 1 and start == n else nc.sync
+                queue.dma_start(out[rows, columns], x[:, columns])

@@ -8,7 +8,7 @@ P = 128
 GROUP = 16
 THRESHOLD = 0.25
 GAIN = 0.5
-LAST_PIECES = (256, 128, 128)
+LAST_PIECES = (256, 128, 64, 64)
 
 
 def tile_lookup_steptanh_out_kernel(tc, tab, offs, out):
@@ -24,17 +24,14 @@ def tile_lookup_steptanh_out_kernel(tc, tab, offs, out):
     ):
         offsets = list_pool.tile([P, offs.shape[1]], U16, name="offsets")
 
-        values, keys = [], []
+        values = [tables.tile([P, places], F32, name="value_tile") for b in range(blocks)]
+        keys = [tables.tile([P, places], F32, name="key_tile") for b in range(blocks)]
+        nc.sync.dma_start(values[0][:], tab[1, :P, :])
+        nc.sync.dma_start(offsets[:], offs)
         for b in range(blocks):
-            rows = slice(b * P, (b + 1) * P)
-            key_tile = tables.tile([P, places], F32, name="key_tile")
-            nc.sync.dma_start(key_tile[:], tab[0, rows, :])
-            if b == 0:
-                nc.sync.dma_start(offsets[:], offs)
-            value_tile = tables.tile([P, places], F32, name="value_tile")
-            nc.sync.dma_start(value_tile[:], tab[1, rows, :])
-            values.append(value_tile)
-            keys.append(key_tile)
+            nc.sync.dma_start(keys[b][:], tab[0, b * P : (b + 1) * P, :])
+        for b in range(1, blocks):
+            nc.sync.dma_start(values[b][:], tab[1, b * P : (b + 1) * P, :])
 
         for b in range(blocks):
             rows = slice(b * P, (b + 1) * P)
@@ -44,12 +41,16 @@ def tile_lookup_steptanh_out_kernel(tc, tab, offs, out):
             )
             squashed = work.tile([P, n], F32, name="squashed")
             x = work.tile([P, n], F32, name="x")
-            start = 0
-            for width in LAST_PIECES if b == blocks - 1 else (n,):
-                columns = slice(start, start + width)
-                entries = offsets[:, start // GROUP : (start + width) // GROUP]
+            widths = LAST_PIECES if b == blocks - 1 else (n,)
+            pieces = [slice(sum(widths[:i]), sum(widths[: i + 1])) for i in range(len(widths))]
+            for columns in pieces:
+                entries = offsets[:, columns.start // GROUP : columns.stop // GROUP]
                 nc.scalar.activation(squashed[:, columns], values[b][:].indirect(entries), TANH)
                 nc.vector.tensor_tensor(x[:, columns], step[:, columns], squashed[:, columns], op=ALU.mult)
-                start += width
-                queue = nc.scalar if b == blocks - 1 and start == n else nc.sync
-                queue.dma_start(out[rows, columns], x[:, columns])
+            if b < blocks - 1:
+                nc.sync.dma_start(out[rows, :], x[:])
+            else:
+                for columns in pieces[:-2]:
+                    nc.sync.dma_start(out[rows, columns], x[:, columns])
+                columns = slice(pieces[-2].start, n)
+                nc.scalar.dma_start(out[rows, columns], x[:, columns])

@@ -26,15 +26,15 @@ def tile_lookup_steptanh_out_kernel(tc, tab, offs, out):
 
         values = [tables.tile([P, places], F32, name="value_tile") for b in range(blocks)]
         keys = [tables.tile([P, places], F32, name="key_tile") for b in range(blocks)]
-        nc.sync.dma_start(values[0][:], tab[1, :P, :])
+        nc.sync.dma_start(values[0][:], tab[1, 0::blocks, :])
         nc.sync.dma_start(offsets[:], offs)
         for b in range(blocks):
-            nc.sync.dma_start(keys[b][:], tab[0, b * P : (b + 1) * P, :])
+            nc.sync.dma_start(keys[b][:], tab[0, b::blocks, :])
         for b in range(1, blocks):
-            nc.sync.dma_start(values[b][:], tab[1, b * P : (b + 1) * P, :])
+            nc.sync.dma_start(values[b][:], tab[1, b::blocks, :])
 
         for b in range(blocks):
-            rows = slice(b * P, (b + 1) * P)
+            rows = slice(b, out.shape[0], blocks)
             step = work.tile([P, n], F32, name="step")
             nc.vector.tensor_scalar(
                 step[:], keys[b][:].indirect(offsets[:]), THRESHOLD, GAIN, op0=ALU.is_ge, op1=ALU.mult

@@ -8,6 +8,7 @@ P = 128
 GROUP = 16
 THRESHOLD = 0.25
 GAIN = 0.5
+BURST = 256
 LAST_PIECES = (256, 128, 64, 64)
 
 
@@ -24,8 +25,8 @@ def tile_lookup_steptanh_out_kernel(tc, tab, offs, out):
     ):
         offsets = list_pool.tile([P, offs.shape[1]], U16, name="offsets")
 
-        values = [tables.tile([P, places], F32, name="value_tile") for b in range(blocks)]
-        keys = [tables.tile([P, places], F32, name="key_tile") for b in range(blocks)]
+        values = [tables.tile([P, places], F32, name="value_tile", align_bytes=BURST) for b in range(blocks)]
+        keys = [tables.tile([P, places], F32, name="key_tile", align_bytes=BURST) for b in range(blocks)]
         nc.sync.dma_start(values[0][:], tab[1, 0::blocks, :])
         nc.sync.dma_start(offsets[:], offs)
         for b in range(blocks):
@@ -40,7 +41,7 @@ def tile_lookup_steptanh_out_kernel(tc, tab, offs, out):
                 step[:], keys[b][:].indirect(offsets[:]), THRESHOLD, GAIN, op0=ALU.is_ge, op1=ALU.mult
             )
             squashed = work.tile([P, n], F32, name="squashed")
-            x = work.tile([P, n], F32, name="x")
+            x = work.tile([P, n], F32, name="x", align_bytes=BURST)
             widths = LAST_PIECES if b == blocks - 1 else (n,)
             pieces = [slice(sum(widths[:i]), sum(widths[: i + 1])) for i in range(len(widths))]
             for columns in pieces:

@@ -8,7 +8,7 @@ P = 128
 GROUP = 16
 THRESHOLD = 0.25
 GAIN = 0.5
-BURST = 256
+BURST = 512
 LAST_PIECES = (256, 128, 64, 64)
 
 
@@ -23,7 +23,7 @@ def tile_lookup_steptanh_out_kernel(tc, tab, offs, out):
         tc.tile_pool(name="tables", bufs=blocks) as tables,
         tc.tile_pool(name="work", bufs=blocks) as work,
     ):
-        offsets = list_pool.tile([P, offs.shape[1]], U16, name="offsets")
+        offsets = list_pool.tile([P, offs.shape[1]], U16, name="offsets", align_bytes=BURST)
 
         values = [tables.tile([P, places], F32, name="value_tile", align_bytes=BURST) for b in range(blocks)]
         keys = [tables.tile([P, places], F32, name="key_tile", align_bytes=BURST) for b in range(blocks)]

@@ -9,49 +9,52 @@ GROUP = 16
 THRESHOLD = 0.25
 GAIN = 0.5
 BURST = 512
-LAST_PIECES = (256, 128, 64, 64)
+PIECES = (256, 128, 64, 64)
+STORES = (256, 128, 128)
+
+
+def cut(widths):
+    return [slice(sum(widths[:i]), sum(widths[: i + 1])) for i in range(len(widths))]
 
 
 def tile_lookup_steptanh_out_kernel(tc, tab, offs, out):
     nc = tc.nc
     places = tab.shape[2]
     n = out.shape[1]
-    blocks = tab.shape[1] // P
+    first, last = slice(0, P), slice(P, 2 * P)
 
-    with (
-        tc.tile_pool(name="list", bufs=1) as list_pool,
-        tc.tile_pool(name="tables", bufs=blocks) as tables,
-        tc.tile_pool(name="work", bufs=blocks) as work,
-    ):
-        offsets = list_pool.tile([P, offs.shape[1]], U16, name="offsets", align_bytes=BURST)
-
-        values = [tables.tile([P, places], F32, name="value_tile", align_bytes=BURST) for b in range(blocks)]
-        keys = [tables.tile([P, places], F32, name="key_tile", align_bytes=BURST) for b in range(blocks)]
-        nc.sync.dma_start(values[0][:], tab[1, 0::blocks, :])
+    with tc.tile_pool(name="held", bufs=1) as held:
+        offsets = held.tile([P, offs.shape[1]], U16, align_bytes=BURST)
+        first_values = held.tile([P, places], F32, align_bytes=BURST)
+        first_keys = held.tile([P, places], F32, align_bytes=BURST)
+        last_keys = held.tile([P, places], F32, align_bytes=BURST)
+        last_values = held.tile([P, places], F32, align_bytes=BURST)
+        nc.sync.dma_start(first_values[:], tab[1, first, :])
         nc.sync.dma_start(offsets[:], offs)
-        for b in range(blocks):
-            nc.sync.dma_start(keys[b][:], tab[0, b::blocks, :])
-        for b in range(1, blocks):
-            nc.sync.dma_start(values[b][:], tab[1, b::blocks, :])
+        nc.sync.dma_start(first_keys[:], tab[0, first, :])
+        nc.sync.dma_start(last_keys[:], tab[0, last, :])
+        nc.sync.dma_start(last_values[:], tab[1, last, :])
 
-        for b in range(blocks):
-            rows = slice(b, out.shape[0], blocks)
-            step = work.tile([P, n], F32, name="step")
+        first_step = held.tile([P, n], F32)
+        last_step = held.tile([P, n], F32)
+        for step, keys in ((first_step, first_keys), (last_step, last_keys)):
             nc.vector.tensor_scalar(
-                step[:], keys[b][:].indirect(offsets[:]), THRESHOLD, GAIN, op0=ALU.is_ge, op1=ALU.mult
+                step[:], keys[:].indirect(offsets[:]), THRESHOLD, GAIN, op0=ALU.is_ge, op1=ALU.mult
             )
-            squashed = work.tile([P, n], F32, name="squashed")
-            x = work.tile([P, n], F32, name="x", align_bytes=BURST)
-            widths = LAST_PIECES if b == blocks - 1 else (n,)
-            pieces = [slice(sum(widths[:i]), sum(widths[: i + 1])) for i in range(len(widths))]
-            for columns in pieces:
-                entries = offsets[:, columns.start // GROUP : columns.stop // GROUP]
-                nc.scalar.activation(squashed[:, columns], values[b][:].indirect(entries), TANH)
-                nc.vector.tensor_tensor(x[:, columns], step[:, columns], squashed[:, columns], op=ALU.mult)
-            if b < blocks - 1:
-                nc.sync.dma_start(out[rows, :], x[:])
-            else:
-                for columns in pieces[:-2]:
-                    nc.sync.dma_start(out[rows, columns], x[:, columns])
-                columns = slice(pieces[-2].start, n)
-                nc.scalar.dma_start(out[rows, columns], x[:, columns])
+
+        first_squashed = held.tile([P, n], F32)
+        first_x = held.tile([P, n], F32, align_bytes=BURST)
+        nc.scalar.activation(first_squashed[:], first_values[:].indirect(offsets[:]), TANH)
+        nc.gpsimd.tensor_tensor(first_x[:], first_step[:], first_squashed[:], op=ALU.mult)
+        nc.gpsimd.dma_start(out[first, :], first_x[:])
+
+        last_squashed = held.tile([P, n], F32)
+        last_x = held.tile([P, n], F32, align_bytes=BURST)
+        for columns in cut(PIECES):
+            entries = offsets[:, columns.start // GROUP : columns.stop // GROUP]
+            nc.scalar.activation(last_squashed[:, columns], last_values[:].indirect(entries), TANH)
+            nc.vector.tensor_tensor(
+                last_x[:, columns], last_step[:, columns], last_squashed[:, columns], op=ALU.mult
+            )
+        for columns in cut(STORES):
+            nc.sync.dma_start(out[last, columns], last_x[:, columns])

@@ -11,6 +11,7 @@ GAIN = 0.5
 BURST = 512
 PIECES = (256, 128, 64, 64)
 STORES = (256, 128, 128)
+FIRST_STORES = 8
 
 
 def cut(widths):
@@ -45,8 +46,9 @@ def tile_lookup_steptanh_out_kernel(tc, tab, offs, out):
         first_squashed = held.tile([P, n], F32)
         first_x = held.tile([P, n], F32, align_bytes=BURST)
         nc.scalar.activation(first_squashed[:], first_values[:].indirect(offsets[:]), TANH)
-        nc.gpsimd.tensor_tensor(first_x[:], first_step[:], first_squashed[:], op=ALU.mult)
-        nc.gpsimd.dma_start(out[first, :], first_x[:])
+        nc.vector.tensor_tensor(first_x[:], first_step[:], first_squashed[:], op=ALU.mult)
+        for columns in cut((n // FIRST_STORES,) * FIRST_STORES):
+            nc.sync.dma_start(out[first, columns], first_x[:, columns])
 
         last_squashed = held.tile([P, n], F32)
         last_x = held.tile([P, n], F32, align_bytes=BURST)

@@ -9,9 +9,8 @@ GROUP = 16
 THRESHOLD = 0.25
 GAIN = 0.5
 BURST = 512
-PIECES = (256, 128, 64, 64)
-STORES = (256, 128, 128)
-FIRST_STORES = 8
+PIECES = (192, 128, 128, 64)
+STORES = (320, 192)
 
 
 def cut(widths):
@@ -47,8 +46,7 @@ def tile_lookup_steptanh_out_kernel(tc, tab, offs, out):
         first_x = held.tile([P, n], F32, align_bytes=BURST)
         nc.scalar.activation(first_squashed[:], first_values[:].indirect(offsets[:]), TANH)
         nc.vector.tensor_tensor(first_x[:], first_step[:], first_squashed[:], op=ALU.mult)
-        for columns in cut((n // FIRST_STORES,) * FIRST_STORES):
-            nc.sync.dma_start(out[first, columns], first_x[:, columns])
+        nc.sync.dma_start(out[first, :], first_x[:])
 
         last_squashed = held.tile([P, n], F32)
         last_x = held.tile([P, n], F32, align_bytes=BURST)

@@ -9,8 +9,8 @@ GROUP = 16
 THRESHOLD = 0.25
 GAIN = 0.5
 BURST = 512
-PIECES = (192, 128, 128, 64)
-STORES = (320, 192)
+PIECES = (256, 192, 64)
+STORES = (256, 256)
 
 
 def cut(widths):

@@ -9,8 +9,8 @@ GROUP = 16
 THRESHOLD = 0.25
 GAIN = 0.5
 BURST = 512
-PIECES = (256, 192, 64)
-STORES = (256, 256)
+PIECES = (256, 128, 64, 64)
+STORES = (256, 128, 128)
 
 
 def cut(widths):
@@ -25,15 +25,18 @@ def tile_lookup_steptanh_out_kernel(tc, tab, offs, out):
 
     with tc.tile_pool(name="held", bufs=1) as held:
         offsets = held.tile([P, offs.shape[1]], U16, align_bytes=BURST)
-        first_values = held.tile([P, places], F32, align_bytes=BURST)
-        first_keys = held.tile([P, places], F32, align_bytes=BURST)
+        first_pair = held.tile([P, 2, places], F32, align_bytes=BURST)
         last_keys = held.tile([P, places], F32, align_bytes=BURST)
         last_values = held.tile([P, places], F32, align_bytes=BURST)
-        nc.sync.dma_start(first_values[:], tab[1, first, :])
+        nc.sync.dma_start(first_pair[:], tab[:, first, :].rearrange("k p s -> p k s"))
         nc.sync.dma_start(offsets[:], offs)
-        nc.sync.dma_start(first_keys[:], tab[0, first, :])
         nc.sync.dma_start(last_keys[:], tab[0, last, :])
         nc.sync.dma_start(last_values[:], tab[1, last, :])
+
+        first_keys = held.tile([P, places], F32)
+        first_values = held.tile([P, places], F32)
+        nc.vector.tensor_copy(first_keys[:], first_pair[:, 0, :])
+        nc.scalar.copy(first_values[:], first_pair[:, 1, :])
 
         first_step = held.tile([P, n], F32)
         last_step = held.tile([P, n], F32)

@@ -21,22 +21,24 @@ def tile_lookup_steptanh_out_kernel(tc, tab, offs, out):
     nc = tc.nc
     places = tab.shape[2]
     n = out.shape[1]
-    first, last = slice(0, P), slice(P, 2 * P)
+    keys_rows = tab[0].rearrange("(p b) s -> p b s", b=2)
+    values_rows = tab[1].rearrange("(p b) s -> p b s", b=2)
+    out_rows = out.rearrange("(p b) j -> p b j", b=2)
 
     with tc.tile_pool(name="held", bufs=1) as held:
         offsets = held.tile([P, offs.shape[1]], U16, align_bytes=BURST)
-        first_pair = held.tile([P, 2, places], F32, align_bytes=BURST)
-        last_keys = held.tile([P, places], F32, align_bytes=BURST)
+        both_keys = held.tile([P, 2, places], F32, align_bytes=BURST)
+        first_values = held.tile([P, places], F32, align_bytes=BURST)
         last_values = held.tile([P, places], F32, align_bytes=BURST)
-        nc.sync.dma_start(first_pair[:], tab[:, first, :].rearrange("k p s -> p k s"))
+        nc.sync.dma_start(both_keys[:], keys_rows)
         nc.sync.dma_start(offsets[:], offs)
-        nc.sync.dma_start(last_keys[:], tab[0, last, :])
-        nc.sync.dma_start(last_values[:], tab[1, last, :])
+        nc.sync.dma_start(first_values[:], values_rows[:, 0, :])
+        nc.sync.dma_start(last_values[:], values_rows[:, 1, :])
 
         first_keys = held.tile([P, places], F32)
-        first_values = held.tile([P, places], F32)
-        nc.vector.tensor_copy(first_keys[:], first_pair[:, 0, :])
-        nc.scalar.copy(first_values[:], first_pair[:, 1, :])
+        last_keys = held.tile([P, places], F32)
+        nc.vector.tensor_copy(first_keys[:], both_keys[:, 0, :])
+        nc.scalar.copy(last_keys[:], both_keys[:, 1, :])
 
         first_step = held.tile([P, n], F32)
         last_step = held.tile([P, n], F32)
@@ -49,7 +51,7 @@ def tile_lookup_steptanh_out_kernel(tc, tab, offs, out):
         first_x = held.tile([P, n], F32, align_bytes=BURST)
         nc.scalar.activation(first_squashed[:], first_values[:].indirect(offsets[:]), TANH)
         nc.vector.tensor_tensor(first_x[:], first_step[:], first_squashed[:], op=ALU.mult)
-        nc.sync.dma_start(out[first, :], first_x[:])
+        nc.sync.dma_start(out_rows[:, 0, :], first_x[:])
 
         last_squashed = held.tile([P, n], F32)
         last_x = held.tile([P, n], F32, align_bytes=BURST)
@@ -60,4 +62,4 @@ def tile_lookup_steptanh_out_kernel(tc, tab, offs, out):
                 last_x[:, columns], last_step[:, columns], last_squashed[:, columns], op=ALU.mult
             )
         for columns in cut(STORES):
-            nc.sync.dma_start(out[last, columns], last_x[:, columns])
+            nc.sync.dma_start(out_rows[:, 1, columns], last_x[:, columns])

@@ -9,8 +9,8 @@ GROUP = 16
 THRESHOLD = 0.25
 GAIN = 0.5
 BURST = 512
-PIECES = (256, 128, 64, 64)
-STORES = (256, 128, 128)
+PIECES = (224, 160, 64, 64)
+STORES = (224, 160, 128)
 
 
 def cut(widths):

@@ -9,8 +9,7 @@ GROUP = 16
 THRESHOLD = 0.25
 GAIN = 0.5
 BURST = 512
-PIECES = (224, 160, 64, 64)
-STORES = (224, 160, 128)
+PIECES = (224, 160, 128)
 
 
 def cut(widths):
@@ -61,5 +60,5 @@ def tile_lookup_steptanh_out_kernel(tc, tab, offs, out):
             nc.vector.tensor_tensor(
                 last_x[:, columns], last_step[:, columns], last_squashed[:, columns], op=ALU.mult
             )
-        for columns in cut(STORES):
+        for columns in cut(PIECES):
             nc.sync.dma_start(out_rows[:, 1, columns], last_x[:, columns])

@@ -10,6 +10,7 @@ THRESHOLD = 0.25
 GAIN = 0.5
 BURST = 512
 PIECES = (224, 160, 128)
+GPSIMD_SHARE = 128
 
 
 def cut(widths):
@@ -49,7 +50,10 @@ def tile_lookup_steptanh_out_kernel(tc, tab, offs, out):
         first_squashed = held.tile([P, n], F32)
         first_x = held.tile([P, n], F32, align_bytes=BURST)
         nc.scalar.activation(first_squashed[:], first_values[:].indirect(offsets[:]), TANH)
-        nc.vector.tensor_tensor(first_x[:], first_step[:], first_squashed[:], op=ALU.mult)
+        for engine, columns in zip((nc.gpsimd, nc.vector), cut((GPSIMD_SHARE, n - GPSIMD_SHARE))):
+            engine.tensor_tensor(
+                first_x[:, columns], first_step[:, columns], first_squashed[:, columns], op=ALU.mult
+            )
         nc.sync.dma_start(out_rows[:, 0, :], first_x[:])
 
         last_squashed = held.tile([P, n], F32)

@@ -57,12 +57,9 @@ def tile_lookup_steptanh_out_kernel(tc, tab, offs, out):
         nc.sync.dma_start(out_rows[:, 0, :], first_x[:])
 
         last_squashed = held.tile([P, n], F32)
-        last_x = held.tile([P, n], F32, align_bytes=BURST)
-        for columns in cut(PIECES):
+        for i, columns in enumerate(reversed(cut(PIECES[::-1]))):
             entries = offsets[:, columns.start // GROUP : columns.stop // GROUP]
+            piece_x = held.tile([P, PIECES[i]], F32, align_bytes=BURST, name=f"last_x{i}")
             nc.scalar.activation(last_squashed[:, columns], last_values[:].indirect(entries), TANH)
-            nc.vector.tensor_tensor(
-                last_x[:, columns], last_step[:, columns], last_squashed[:, columns], op=ALU.mult
-            )
-        for columns in cut(PIECES):
-            nc.sync.dma_start(out_rows[:, 1, columns], last_x[:, columns])
+            nc.vector.tensor_tensor(piece_x[:], last_step[:, columns], last_squashed[:, columns], op=ALU.mult)
+            nc.sync.dma_start(out_rows[:, 1, columns], piece_x[:])

import concourse.mybir as mybir

F32, U16 = mybir.dt.float32, mybir.dt.uint16
ALU = mybir.AluOpType
TANH = mybir.ActivationFunctionType.Tanh

P = 128
GROUP = 16
THRESHOLD = 0.25
GAIN = 0.5
BURST = 512
PIECES = (224, 160, 128)
GPSIMD_SHARE = 128


def cut(widths):
    return [slice(sum(widths[:i]), sum(widths[: i + 1])) for i in range(len(widths))]


def tile_lookup_steptanh_out_kernel(tc, tab, offs, out):
    nc = tc.nc
    places = tab.shape[2]
    n = out.shape[1]
    keys_rows = tab[0].rearrange("(p b) s -> p b s", b=2)
    values_rows = tab[1].rearrange("(p b) s -> p b s", b=2)
    out_rows = out.rearrange("(p b) j -> p b j", b=2)

    with tc.tile_pool(name="held", bufs=1) as held:
        offsets = held.tile([P, offs.shape[1]], U16, align_bytes=BURST)
        both_keys = held.tile([P, 2, places], F32, align_bytes=BURST)
        first_values = held.tile([P, places], F32, align_bytes=BURST)
        last_values = held.tile([P, places], F32, align_bytes=BURST)
        nc.sync.dma_start(both_keys[:], keys_rows)
        nc.sync.dma_start(offsets[:], offs)
        nc.sync.dma_start(first_values[:], values_rows[:, 0, :])
        nc.sync.dma_start(last_values[:], values_rows[:, 1, :])

        first_keys = held.tile([P, places], F32)
        last_keys = held.tile([P, places], F32)
        nc.vector.tensor_copy(first_keys[:], both_keys[:, 0, :])
        nc.scalar.copy(last_keys[:], both_keys[:, 1, :])

        first_step = held.tile([P, n], F32)
        last_step = held.tile([P, n], F32)
        for step, keys in ((first_step, first_keys), (last_step, last_keys)):
            nc.vector.tensor_scalar(
                step[:], keys[:].indirect(offsets[:]), THRESHOLD, GAIN, op0=ALU.is_ge, op1=ALU.mult
            )

        first_squashed = held.tile([P, n], F32)
        first_x = held.tile([P, n], F32, align_bytes=BURST)
        nc.scalar.activation(first_squashed[:], first_values[:].indirect(offsets[:]), TANH)
        for engine, columns in zip((nc.gpsimd, nc.vector), cut((GPSIMD_SHARE, n - GPSIMD_SHARE))):
            engine.tensor_tensor(
                first_x[:, columns], first_step[:, columns], first_squashed[:, columns], op=ALU.mult
            )
        nc.sync.dma_start(out_rows[:, 0, :], first_x[:])

        last_squashed = held.tile([P, n], F32)
        for i, columns in enumerate(reversed(cut(PIECES[::-1]))):
            entries = offsets[:, columns.start // GROUP : columns.stop // GROUP]
            piece_x = held.tile([P, PIECES[i]], F32, align_bytes=BURST, name=f"last_x{i}")
            nc.scalar.activation(last_squashed[:, columns], last_values[:].indirect(entries), TANH)
            nc.vector.tensor_tensor(piece_x[:], last_step[:, columns], last_squashed[:, columns], op=ALU.mult)
            nc.sync.dma_start(out_rows[:, 1, columns], piece_x[:])
